import numpy as np
import ml_dtypes


def mxq(x, axis, fmt="e4m3"):
    dtype, down = {"e4m3": (ml_dtypes.float8_e4m3fn, 7), "e5m2": (ml_dtypes.float8_e5m2, 14)}[fmt]
    v = np.moveaxis(np.asarray(x, np.float32).astype(ml_dtypes.bfloat16).astype(np.float64), axis, -1)
    blocks = v.reshape(v.shape[:-1] + (-1, 32))
    amax = np.abs(blocks).max(-1, keepdims=True)
    byte = np.maximum(np.where(amax > 0, np.frexp(amax)[1] - 1 + 127, 0) - down, 1)
    scale = np.exp2(byte - 127.0)
    codes = (blocks / scale).astype(np.float32).astype(dtype).astype(np.float64)
    return np.moveaxis((codes * scale).reshape(v.shape), -1, axis)


WIDE = False


def mx_kscale(k):
    if not WIDE:
        return np.ones(k)
    levels = np.array([10, -10, 5, -5, 0])
    if k % 512:
        return np.exp2(np.random.permutation(np.resize(levels, k // 32))).repeat(32)
    a = np.empty((k // 512, 16))
    for p in range(k // 512):
        a[p, :8] = np.random.permutation(np.resize(levels, 8))
        for g in range(8):
            far = levels[np.abs(levels - a[p, g]) >= 10]
            a[p, g + 8] = far[np.random.randint(len(far))]
    return np.exp2(a.ravel()).repeat(32)


def f64(x):
    return np.asarray(x).astype(np.float64)


def striped(idx):
    return np.tile(idx.reshape(-1, 16).T, (8, 1)).astype(np.uint16)


def unstriped(offs):
    return offs[:16].T.reshape(-1).astype(np.int64)


def striped8(idx):
    return np.concatenate([x.reshape(-1, 16).T for x in idx]).astype(np.uint16)


def runs(offs, k):
    lists = np.stack([offs[16 * r : 16 * r + 16].T.reshape(-1) for r in range(8)]).astype(np.int64)
    return lists[np.arange(k) % 512 // 64]


def pack_weight(w):
    k, n = w.shape
    w = f64(np.asarray(w, np.float32).astype(ml_dtypes.bfloat16)).reshape(k // 32, 32, n)
    amax = np.abs(w).max(1)
    byte = np.clip(np.where(amax > 0, np.frexp(amax)[1] - 1 + 127 - 7, 1), 1, 254)
    scaled = (w * np.exp2(127.0 - byte)[:, None, :]).reshape(k, n).astype(np.float32)
    words = np.ascontiguousarray(scaled.reshape(k // 512, 128, 4, n).transpose(0, 1, 3, 2)).astype(ml_dtypes.float8_e4m3fn).view(np.uint8)
    return words, np.ascontiguousarray(byte.astype(np.uint8).reshape(k // 512, 16, n))


def unpack_weight(words, scales):
    g, p, n, _ = words.shape
    vals = np.ascontiguousarray(words).view(ml_dtypes.float8_e4m3fn).astype(np.float64) * np.repeat(np.exp2(scales.astype(np.float64) - 127.0), 8, axis=1)[..., None]
    return vals.transpose(0, 1, 3, 2).reshape(g * 512, n)


K, T, S, H, G, W = 512, 1024, 512, 512, 2048, 256


def setup_inputs():
    n = np.random.standard_normal
    s = mx_kscale(K)[:, None]
    packed_xT = pack_weight(n((K, T)) * s)
    packed_dT = pack_weight(n((K, G)) / s)
    perm = np.stack([np.random.permutation(S) for _ in range(8)])
    return {
        "x_words": packed_xT[0],
        "x_scales": packed_xT[1],
        "w1": (n((K, H)) / np.sqrt(K) / s).astype(np.float32),
        "w2": (n((K, H)) / np.sqrt(K) / s).astype(np.float32),
        "gs": (np.random.uniform(0.5, 1.5, (K, 1)) * s).astype(np.float32),
        "d_words": packed_dT[0],
        "d_scales": packed_dT[1],
        "offs": striped(np.random.permutation(T)[:S]),
        "two": striped(np.random.permutation(T)[:S]),
        "n1": striped8(np.stack([np.random.permutation(S) for _ in range(8)])),
        "n2": striped8(np.stack([np.random.permutation(S) for _ in range(8)])),
        "k1": striped8(np.random.randint(0, G, (8, H))),
        "n3": striped8(perm[:, :W]),
        "n4": striped8(perm[:, W:]),
    }


def reference(x_words, x_scales, w1, w2, gs, d_words, d_scales, offs, two, n1, n2, k1, n3, n4):
    d_k1 = unpack_weight(d_words, d_scales)[np.arange(K)[:, None], runs(k1, K)]
    xq = unpack_weight(x_words, x_scales)[:, unstriped(offs)]
    y = mxq(f64(w1), 0, "e4m3").T @ xq
    x_two = unpack_weight(x_words, x_scales)[:, unstriped(two)]
    d = mxq(f64(w2), 0, "e4m3").T @ x_two
    z = f64(gs) * (y * (np.tanh(d[np.arange(H)[:, None], runs(n1, H)] - (d[np.arange(H)[:, None], runs(n2, H)]))))
    h = 0.0625 * ((d_k1.T @ mxq(z, 0, "e4m3")))
    pb = h[np.arange(H)[:, None], runs(n4, H)]
    pa = h[np.arange(H)[:, None], runs(n3, H)]
    rb = pb - (0.5 * pa)
    ra = np.sqrt((pa) ** 2 + (pb) ** 2 + 0.25)
    ds = np.zeros((H, S))
    ds[np.arange(H)[:, None], runs(n3, H)] = ra
    out = ds.copy()
    out[np.arange(H)[:, None], runs(n4, H)] = rb
    return out

@@ -1,0 +1,212 @@
+from contextlib import ExitStack
+
+import concourse.mybir as mybir
+
+F32 = mybir.dt.float32
+BF16 = mybir.dt.bfloat16
+I32 = mybir.dt.int32
+U32 = mybir.dt.uint32
+U16 = mybir.dt.uint16
+U8 = mybir.dt.uint8
+FP8X4 = mybir.dt.float8_e4m3fn_x4
+ALU = mybir.AluOpType
+ACT = mybir.ActivationFunctionType
+
+K, T, S, H, G, W = 512, 1024, 512, 512, 2048, 256
+P = 128
+PACK = 4
+Z_CHUNK = 256
+FLOPS = 3 * 2 * K * H * S
+
+
+def tile_picked_twqjointbpolar_none_p_kernel(
+    tc, x_words, x_scales, w1, w2, gs, d_words, d_scales, offs, two, n1, n2, k1, n3, n4, out
+):
+    nc = tc.nc
+    with ExitStack() as ctx:
+        keep = ctx.enter_context(tc.tile_pool(name="keep", bufs=1))
+        psum = ctx.enter_context(tc.psum_pool(name="psum", bufs=1))
+
+        def sb(name, shape, dtype, tag=""):
+            return keep.tile(shape, dtype, name=name, tag=tag, align_bytes=64)
+
+        def load_list(name, src):
+            tile = keep.tile(list(src.shape), U16, name=name)
+            nc.sync.dma_start(tile[:], src)
+            return tile
+
+        def load_half(name, w, half):
+            raw = sb(name, [P, PACK, H // 2], F32)
+            cols = slice(half * H // 2, (half + 1) * H // 2)
+            nc.sync.dma_start(raw[:], w[:, cols].rearrange("(p j) c -> p j c", j=PACK))
+            return raw
+
+        xs_table = sb("xs_table", [P, T], U8)
+        nc.gpsimd.memset(xs_table[:].bitcast(I32), 0)
+        ds_table = sb("ds_table", [P, G], U8)
+        nc.vector.memset(ds_table[:].bitcast(I32), 0)
+        dq_scales = sb("dq_scales", [P, H], U8)
+        nc.vector.memset(dq_scales[:].bitcast(I32), 0)
+        d_win = [sb("d_win%d" % a, [P, 2 * S], F32) for a in range(2)]
+        for win in d_win:
+            nc.vector.memset(win[:, S:], 0.0)
+        sq_win = [sb("sq_win%d" % a, [P, S], F32) for a in range(2)]
+        for win in sq_win:
+            nc.vector.memset(win[:], 0.0)
+
+        two_l = load_list("two_l", two)
+        for q in range(4):
+            nc.scalar.dma_start(xs_table[32 * q : 32 * q + 4, :].bitcast(I32), x_scales[0, 4 * q : 4 * q + 4, :].bitcast(I32))
+        xw_table = sb("xw_table", [P, T], I32)
+        nc.sync.dma_start(xw_table[:], x_words[0].rearrange("p n t -> p (n t)").bitcast(I32))
+        offs_l = load_list("offs_l", offs)
+        w2_raw = [load_half("w2_raw%d" % a, w2, a) for a in range(2)]
+        k1_l = load_list("k1_l", k1)
+        for e in range(2):
+            nc.sync.dma_start(ds_table[e:P:16, :].bitcast(I32), d_scales[0, e:16:2, :].bitcast(I32))
+        n2_l = load_list("n2_l", n2)
+        n1_l = load_list("n1_l", n1)
+        w1_raw = [load_half("w1_raw%d" % a, w1, a) for a in range(2)]
+        gs_t = sb("gs_t", [P, PACK], F32)
+        nc.sync.dma_start(gs_t[:], gs.rearrange("(p t) o -> p (t o)", t=PACK))
+        dw_table = sb("dw_table", [P, G], I32)
+        nc.sync.dma_start(dw_table[:], d_words[0].rearrange("p n t -> p (n t)").bitcast(I32))
+        n3_l = load_list("n3_l", n3)
+        n4_l = load_list("n4_l", n4)
+
+        def round_weights(name, raws):
+            grouped = sb(name, [P, H * PACK], BF16, name)
+            view = grouped[:].rearrange("p (t m j) -> p m j t", t=PACK, j=PACK)
+            for half, raw in enumerate(raws):
+                nc.scalar.copy(view[:, half * 64 : (half + 1) * 64], raw[:].rearrange("p j (m t) -> p m j t", t=PACK))
+            return grouped
+
+        def quantise(name, values):
+            n = values.shape[1] // PACK
+            codes = sb(name + "_codes", [P, n], U32)
+            scales = sb(name + "_scales", [P, n], U8)
+            nc.vector.quantize_mx(out=codes[:].bitcast(FP8X4), scales=scales[:], in_=values[:])
+            return codes, scales
+
+        def gather(name, table, lst, dtype, tag=""):
+            picked = sb(name, [P, lst.shape[1] * 16], dtype, tag)
+            nc.vector.tensor_copy(picked[:], table.indirect(lst[:]))
+            return picked
+
+        def product(acc, lhs, t, rhs):
+            cols = slice(t * P, (t + 1) * P)
+            nc.tensor.matmul_mx(
+                out=acc,
+                lhsT=lhs[0][:, cols].bitcast(FP8X4),
+                lhsT_scale=lhs[1][:, cols],
+                rhs=rhs[0][:].bitcast(FP8X4),
+                rhs_scale=rhs[1][:],
+                start=True,
+                stop=True,
+            )
+
+        def bank(name, b):
+            return psum.tile([P, S], F32, name=name, tag="bank%d" % b)
+
+        xs_two = gather("xs_two", xs_table[:], two_l, U8)
+        xs_offs = gather("xs_offs", xs_table[:], offs_l, U8)
+        xw_two = gather("xw_two", xw_table[:].bitcast(U32), two_l, U32)
+        xw_offs = gather("xw_offs", xw_table[:].bitcast(U32), offs_l, U32)
+        w2_q = quantise("w2", round_weights("w2_bf", w2_raw))
+        d_ps = [bank("d_ps%d" % t, t) for t in range(PACK)]
+        for t in range(PACK):
+            product(d_ps[t][:], w2_q, t, (xw_two, xs_two))
+
+        ds_picked = gather("ds_picked", ds_table[:], k1_l, U8, "w2_bf")
+        ds_dealt = sb("ds_dealt", [P, H], U8)
+        nc.vector.tensor_copy(
+            ds_dealt[:].bitcast(I32).rearrange("p (t a b) -> p t a b", t=PACK, b=2),
+            ds_picked[:].bitcast(I32).rearrange("p (a t b) -> p t a b", t=PACK, b=2),
+        )
+        for odd in range(2):
+            for e in range(2):
+                nc.sync.dma_start(dq_scales[2 * odd + e : P : 32, :].bitcast(I32), ds_dealt[16 * odd + e : P : 32, :].bitcast(I32))
+
+        th = sb("th", [P, PACK, S], F32)
+        yg = sb("yg", [P, PACK, S], F32)
+        for t in range(PACK):
+            win = d_win[t % 2]
+            nc.scalar.copy(win[:, :S], d_ps[t][:])
+            d2 = gather("d2_%d" % t, win[:], n2_l, F32, "d2_%d" % (t % 2))
+            diff = sb("diff%d" % t, [P, S], F32)
+            nc.vector.tensor_tensor(diff[:], win[:].indirect(n1_l[:]), d2[:], ALU.subtract)
+            nc.scalar.activation(th[:, t, :], diff[:], ACT.Tanh)
+            if t == 0:
+                w1_q = quantise("w1", round_weights("w1_bf", w1_raw))
+                for u in range(PACK):
+                    y_ps = bank("y_ps%d" % u, PACK + u)
+                    product(y_ps[:], w1_q, u, (xw_offs, xs_offs))
+                    nc.scalar.activation(yg[:, u, :], y_ps[:], ACT.Copy, scale=gs_t[:, u : u + 1])
+
+        dw_picked = gather("dw_picked", dw_table[:].bitcast(U32), k1_l, U32, "d2_1")
+        dq_codes = sb("dq_codes", [P, H], U32)
+        nc.vector.tensor_copy(
+            dq_codes[:].rearrange("p (t a b) -> p t a b", t=PACK, b=8),
+            dw_picked[:].rearrange("p (a t b) -> p t a b", t=PACK, b=8),
+        )
+
+        chunks = [slice(c, c + Z_CHUNK) for c in range(0, S, Z_CHUNK)]
+        z_bf = []
+        for c, cols in enumerate(chunks):
+            zb = sb("z_bf%d" % c, [P, Z_CHUNK * PACK], BF16)
+            nc.vector.tensor_tensor(
+                zb[:].rearrange("p (c i t) -> p c t i", i=4, t=PACK),
+                yg[:, :, cols].rearrange("p t (c i) -> p c t i", i=4),
+                th[:, :, cols].rearrange("p t (c i) -> p c t i", i=4),
+                ALU.mult,
+            )
+            z_bf.append(zb)
+        z_q = [quantise("z%d" % c, zb) for c, zb in enumerate(z_bf)]
+
+        h_ps = [bank("h_ps%d" % t, t) for t in range(PACK)]
+        h0_late = bank("h0_late", PACK)
+        h_win = [sb("h_win%d" % t, [P, S], F32) for t in range(PACK)]
+        for c, cols in enumerate(chunks):
+            for t in range(PACK):
+                acc = h0_late if (t == 0 and c == 1) else h_ps[t]
+                product(acc[:, cols], (dq_codes, dq_scales), t, z_q[c])
+                if t == 0:
+                    nc.scalar.activation(h_win[0][:, cols], acc[:, cols], ACT.Copy, scale=0.0625)
+
+        out_v = out.rearrange("(a t b) n -> t a b n", t=PACK, b=8)
+        pairs = []
+
+        def fetch(t):
+            if t > 0:
+                nc.scalar.activation(h_win[t][:], h_ps[t][:], ACT.Copy, scale=0.0625)
+            half_a = sb("half_a%d" % t, [P, W], F32)
+            nc.vector.tensor_scalar(half_a[:], h_win[t][:].indirect(n3_l[:]), -0.5, 0.0, ALU.mult, ALU.add)
+            pb = gather("pb%d" % t, h_win[t][:], n4_l, F32)
+            pairs.append((half_a, pb))
+
+        results = []
+
+        def root(t):
+            half_a, pb = pairs[t]
+            sq_a = sb("sq_a%d" % t, [P, W], F32)
+            sq_b = sb("sq_b%d" % t, [P, W], F32)
+            nc.scalar.activation(sq_a[:], half_a[:], ACT.Square, scale=2.0)
+            nc.scalar.activation(sq_b[:], pb[:], ACT.Square)
+            win = sq_win[t % 2]
+            nc.vector.tensor_tensor(win[:].indirect(n3_l[:]), sq_a[:], sq_b[:], ALU.add)
+            res = sb("res%d" % t, [P, S], F32)
+            nc.scalar.activation(res[:], win[:], ACT.Sqrt, bias=0.25)
+            results.append(res)
+
+        def finish(t):
+            half_a, pb = pairs[t]
+            nc.vector.tensor_tensor(results[t][:].indirect(n4_l[:]), pb[:], half_a[:], ALU.add)
+            nc.sync.dma_start(out_v[t], results[t][:])
+
+        for step in range(PACK + 2):
+            if step < PACK:
+                fetch(step)
+            if 1 <= step <= PACK:
+                root(step - 1)
+            if step >= 2:
+                finish(step - 2)

@@ -1,6 +1,7 @@
 from contextlib import ExitStack
 
 import concourse.mybir as mybir
+from concourse.masks import make_identity
 
 F32 = mybir.dt.float32
 BF16 = mybir.dt.bfloat16
@@ -15,7 +16,6 @@ ACT = mybir.ActivationFunctionType
 K, T, S, H, G, W = 512, 1024, 512, 512, 2048, 256
 P = 128
 PACK = 4
-Z_CHUNK = 256
 FLOPS = 3 * 2 * K * H * S
 
 
@@ -42,31 +42,35 @@ def tile_picked_twqjointbpolar_none_p_kernel(
             return raw
 
         xs_table = sb("xs_table", [P, T], U8)
-        nc.gpsimd.memset(xs_table[:].bitcast(I32), 0)
+        nc.vector.memset(xs_table[:].bitcast(I32), 0)
         ds_table = sb("ds_table", [P, G], U8)
         nc.vector.memset(ds_table[:].bitcast(I32), 0)
         dq_scales = sb("dq_scales", [P, H], U8)
         nc.vector.memset(dq_scales[:].bitcast(I32), 0)
-        d_win = [sb("d_win%d" % a, [P, 2 * S], F32) for a in range(2)]
+        d_win = [sb("d_win%d" % a, [P, 2 * S], F32, "d_win%d" % a) for a in range(2)]
         for win in d_win:
             nc.vector.memset(win[:, S:], 0.0)
         sq_win = [sb("sq_win%d" % a, [P, S], F32) for a in range(2)]
         for win in sq_win:
             nc.vector.memset(win[:], 0.0)
 
+        ident = sb("ident", [P, P], F32)
+        make_identity(nc, ident[:])
+
         two_l = load_list("two_l", two)
+        offs_l = load_list("offs_l", offs)
         for q in range(4):
-            nc.scalar.dma_start(xs_table[32 * q : 32 * q + 4, :].bitcast(I32), x_scales[0, 4 * q : 4 * q + 4, :].bitcast(I32))
+            queue = nc.sync if q < 2 else nc.scalar
+            queue.dma_start(xs_table[32 * q : 32 * q + 4, :].bitcast(I32), x_scales[0, 4 * q : 4 * q + 4, :].bitcast(I32))
         xw_table = sb("xw_table", [P, T], I32)
         nc.sync.dma_start(xw_table[:], x_words[0].rearrange("p n t -> p (n t)").bitcast(I32))
-        offs_l = load_list("offs_l", offs)
         w2_raw = [load_half("w2_raw%d" % a, w2, a) for a in range(2)]
         k1_l = load_list("k1_l", k1)
         for e in range(2):
             nc.sync.dma_start(ds_table[e:P:16, :].bitcast(I32), d_scales[0, e:16:2, :].bitcast(I32))
+        w1_raw = [load_half("w1_raw%d" % a, w1, a) for a in range(2)]
         n2_l = load_list("n2_l", n2)
         n1_l = load_list("n1_l", n1)
-        w1_raw = [load_half("w1_raw%d" % a, w1, a) for a in range(2)]
         gs_t = sb("gs_t", [P, PACK], F32)
         nc.sync.dma_start(gs_t[:], gs.rearrange("(p t) o -> p (t o)", t=PACK))
         dw_table = sb("dw_table", [P, G], I32)
@@ -99,8 +103,8 @@ def tile_picked_twqjointbpolar_none_p_kernel(
                 out=acc,
                 lhsT=lhs[0][:, cols].bitcast(FP8X4),
                 lhsT_scale=lhs[1][:, cols],
-                rhs=rhs[0][:].bitcast(FP8X4),
-                rhs_scale=rhs[1][:],
+                rhs=rhs[0].bitcast(FP8X4),
+                rhs_scale=rhs[1],
                 start=True,
                 stop=True,
             )
@@ -115,7 +119,7 @@ def tile_picked_twqjointbpolar_none_p_kernel(
         w2_q = quantise("w2", round_weights("w2_bf", w2_raw))
         d_ps = [bank("d_ps%d" % t, t) for t in range(PACK)]
         for t in range(PACK):
-            product(d_ps[t][:], w2_q, t, (xw_two, xs_two))
+            product(d_ps[t][:], w2_q, t, (xw_two[:], xs_two[:]))
 
         ds_picked = gather("ds_picked", ds_table[:], k1_l, U8, "w2_bf")
         ds_dealt = sb("ds_dealt", [P, H], U8)
@@ -127,51 +131,83 @@ def tile_picked_twqjointbpolar_none_p_kernel(
             for e in range(2):
                 nc.sync.dma_start(dq_scales[2 * odd + e : P : 32, :].bitcast(I32), ds_dealt[16 * odd + e : P : 32, :].bitcast(I32))
 
-        th = sb("th", [P, PACK, S], F32)
+        w1_q = quantise("w1", round_weights("w1_bf", w1_raw))
+        for t in range(2):
+            nc.scalar.copy(d_win[t][:, :S], d_ps[t][:])
         yg = sb("yg", [P, PACK, S], F32)
         for t in range(PACK):
-            win = d_win[t % 2]
-            nc.scalar.copy(win[:, :S], d_ps[t][:])
-            d2 = gather("d2_%d" % t, win[:], n2_l, F32, "d2_%d" % (t % 2))
-            diff = sb("diff%d" % t, [P, S], F32)
-            nc.vector.tensor_tensor(diff[:], win[:].indirect(n1_l[:]), d2[:], ALU.subtract)
-            nc.scalar.activation(th[:, t, :], diff[:], ACT.Tanh)
-            if t == 0:
-                w1_q = quantise("w1", round_weights("w1_bf", w1_raw))
-                for u in range(PACK):
-                    y_ps = bank("y_ps%d" % u, PACK + u)
-                    product(y_ps[:], w1_q, u, (xw_offs, xs_offs))
-                    nc.scalar.activation(yg[:, u, :], y_ps[:], ACT.Copy, scale=gs_t[:, u : u + 1])
+            y_ps = bank("y_ps%d" % t, PACK + t)
+            product(y_ps[:], w1_q, t, (xw_offs[:], xs_offs[:]))
+            nc.scalar.activation(yg[:, t, :], y_ps[:], ACT.Copy, scale=gs_t[:, t : t + 1])
 
-        dw_picked = gather("dw_picked", dw_table[:].bitcast(U32), k1_l, U32, "d2_1")
+        yg_woven = [sb("yg_woven%d" % c, [P, P, PACK], F32) for c in range(S // P)]
+        to_weave = list(range(S // P))
+
+        def weave():
+            c = to_weave[0]
+            to_weave.remove(c)
+            nc.scalar.copy(yg_woven[c][:], yg[:, :, c * P : (c + 1) * P].rearrange("p t j -> p j t"))
+
+        th_ps = [bank("th_ps%d" % c, PACK + c) for c in range(S // P)]
+        pieces = [(t, 0, S) for t in range(PACK - 1)] + [(PACK - 1, 0, S // 2), (PACK - 1, S // 2, S)]
+        for n, (t, lo, hi) in enumerate(pieces):
+            win = d_win[t % 2]
+            entries = slice(lo // 16, hi // 16)
+            minus = sb("minus%d" % n, [P, hi - lo], F32)
+            nc.vector.tensor_scalar(minus[:], win[:].indirect(n2_l[:, entries]), -1.0, 0.0, ALU.mult, ALU.add)
+            plus = sb("plus%d" % n, [P, hi - lo], F32)
+            nc.vector.tensor_copy(plus[:], win[:].indirect(n1_l[:, entries]))
+            if n in (1, 2):
+                weave()
+            if t + 2 < PACK:
+                nc.scalar.copy(win[:, :S], d_ps[t + 2][:])
+            diff_ps = bank("diff_ps%d" % n, n % PACK)
+            for c in range(0, hi - lo, P):
+                for term, first in ((minus, True), (plus, False)):
+                    nc.tensor.matmul(diff_ps[:, c : c + P], term[:, c : c + P], ident[:], start=first, stop=not first, is_transpose=True)
+            if n in (1, 2):
+                weave()
+            turned = sb("turned%d" % n, [P, hi - lo], F32)
+            nc.scalar.activation(turned[:], diff_ps[:, : hi - lo], ACT.Tanh)
+            for c in range(0, hi - lo, P):
+                nc.tensor.transpose(th_ps[(lo + c) // P][:, t * P : (t + 1) * P], turned[:, c : c + P], ident[:])
+
+        dw_picked = gather("dw_picked", dw_table[:].bitcast(U32), k1_l, U32, "d_win1")
         dq_codes = sb("dq_codes", [P, H], U32)
         nc.vector.tensor_copy(
             dq_codes[:].rearrange("p (t a b) -> p t a b", t=PACK, b=8),
             dw_picked[:].rearrange("p (a t b) -> p t a b", t=PACK, b=8),
         )
 
-        chunks = [slice(c, c + Z_CHUNK) for c in range(0, S, Z_CHUNK)]
-        z_bf = []
-        for c, cols in enumerate(chunks):
-            zb = sb("z_bf%d" % c, [P, Z_CHUNK * PACK], BF16)
+        z_bf = sb("z_bf", [P, S * PACK], BF16)
+        z_codes = sb("z_codes", [P, S], U32)
+        z_scales = sb("z_scales", [P, S], U8)
+        h_win = [sb("h_win%d" % t, [P, S], F32) for t in range(PACK)]
+        dq = (dq_codes, dq_scales)
+
+        def multiply(c):
             nc.vector.tensor_tensor(
-                zb[:].rearrange("p (c i t) -> p c t i", i=4, t=PACK),
-                yg[:, :, cols].rearrange("p t (c i) -> p c t i", i=4),
-                th[:, :, cols].rearrange("p t (c i) -> p c t i", i=4),
+                z_bf[:, c * P * PACK : (c + 1) * P * PACK].rearrange("p (j t) -> p j t", t=PACK),
+                th_ps[c][:].rearrange("p (t j) -> p j t", t=PACK),
+                yg_woven[c][:],
                 ALU.mult,
             )
-            z_bf.append(zb)
-        z_q = [quantise("z%d" % c, zb) for c, zb in enumerate(z_bf)]
 
-        h_ps = [bank("h_ps%d" % t, t) for t in range(PACK)]
-        h0_late = bank("h0_late", PACK)
-        h_win = [sb("h_win%d" % t, [P, S], F32) for t in range(PACK)]
-        for c, cols in enumerate(chunks):
-            for t in range(PACK):
-                acc = h0_late if (t == 0 and c == 1) else h_ps[t]
-                product(acc[:, cols], (dq_codes, dq_scales), t, z_q[c])
-                if t == 0:
-                    nc.scalar.activation(h_win[0][:, cols], acc[:, cols], ACT.Copy, scale=0.0625)
+        def first_rows(n, lo, hi):
+            nc.vector.quantize_mx(out=z_codes[:, lo:hi].bitcast(FP8X4), scales=z_scales[:, lo:hi], in_=z_bf[:, lo * PACK : hi * PACK])
+            acc = bank("h0_ps%d" % n, PACK + n)
+            product(acc[:, : hi - lo], dq, 0, (z_codes[:, lo:hi], z_scales[:, lo:hi]))
+            nc.scalar.activation(h_win[0][:, lo:hi], acc[:, : hi - lo], ACT.Copy, scale=0.0625)
+
+        for c in range(3):
+            multiply(c)
+        first_rows(0, 0, 2 * P)
+        multiply(3)
+        first_rows(1, 2 * P, 3 * P)
+        first_rows(2, 3 * P, 4 * P)
+        h_ps = [None] + [bank("h_ps%d" % t, t) for t in range(1, PACK)]
+        for t in range(1, PACK):
+            product(h_ps[t][:], dq, t, (z_codes[:], z_scales[:]))
 
         out_v = out.rearrange("(a t b) n -> t a b n", t=PACK, b=8)
         pairs = []

@@ -1,7 +1,6 @@
 from contextlib import ExitStack
 
 import concourse.mybir as mybir
-from concourse.masks import make_identity
 
 F32 = mybir.dt.float32
 BF16 = mybir.dt.bfloat16
@@ -53,9 +52,6 @@ def tile_picked_twqjointbpolar_none_p_kernel(
         sq_win = [sb("sq_win%d" % a, [P, S], F32) for a in range(2)]
         for win in sq_win:
             nc.vector.memset(win[:], 0.0)
-
-        ident = sb("ident", [P, P], F32)
-        make_identity(nc, ident[:])
 
         two_l = load_list("two_l", two)
         offs_l = load_list("offs_l", offs)
@@ -140,37 +136,20 @@ def tile_picked_twqjointbpolar_none_p_kernel(
             product(y_ps[:], w1_q, t, (xw_offs[:], xs_offs[:]))
             nc.scalar.activation(yg[:, t, :], y_ps[:], ACT.Copy, scale=gs_t[:, t : t + 1])
 
-        yg_woven = [sb("yg_woven%d" % c, [P, P, PACK], F32) for c in range(S // P)]
-        to_weave = list(range(S // P))
-
-        def weave():
-            c = to_weave[0]
-            to_weave.remove(c)
-            nc.scalar.copy(yg_woven[c][:], yg[:, :, c * P : (c + 1) * P].rearrange("p t j -> p j t"))
-
-        th_ps = [bank("th_ps%d" % c, PACK + c) for c in range(S // P)]
-        pieces = [(t, 0, S) for t in range(PACK - 1)] + [(PACK - 1, 0, S // 2), (PACK - 1, S // 2, S)]
-        for n, (t, lo, hi) in enumerate(pieces):
+        blocks = [slice(c, c + P) for c in range(0, S, P)]
+        yg_woven = [sb("yg_woven%d" % c, [P, P, PACK], F32) for c in range(len(blocks))]
+        diff = sb("diff", [P, PACK, S], F32)
+        for t in range(PACK):
             win = d_win[t % 2]
-            entries = slice(lo // 16, hi // 16)
-            minus = sb("minus%d" % n, [P, hi - lo], F32)
-            nc.vector.tensor_scalar(minus[:], win[:].indirect(n2_l[:, entries]), -1.0, 0.0, ALU.mult, ALU.add)
-            plus = sb("plus%d" % n, [P, hi - lo], F32)
-            nc.vector.tensor_copy(plus[:], win[:].indirect(n1_l[:, entries]))
-            if n in (1, 2):
-                weave()
+            d2 = gather("d2_%d" % t, win[:], n2_l, F32)
+            nc.vector.tensor_tensor(diff[:, t, :], win[:].indirect(n1_l[:]), d2[:], ALU.subtract)
             if t + 2 < PACK:
                 nc.scalar.copy(win[:, :S], d_ps[t + 2][:])
-            diff_ps = bank("diff_ps%d" % n, n % PACK)
-            for c in range(0, hi - lo, P):
-                for term, first in ((minus, True), (plus, False)):
-                    nc.tensor.matmul(diff_ps[:, c : c + P], term[:, c : c + P], ident[:], start=first, stop=not first, is_transpose=True)
-            if n in (1, 2):
-                weave()
-            turned = sb("turned%d" % n, [P, hi - lo], F32)
-            nc.scalar.activation(turned[:], diff_ps[:, : hi - lo], ACT.Tanh)
-            for c in range(0, hi - lo, P):
-                nc.tensor.transpose(th_ps[(lo + c) // P][:, t * P : (t + 1) * P], turned[:, c : c + P], ident[:])
+                for c in (2 * t, 2 * t + 1):
+                    nc.scalar.copy(yg_woven[c][:], yg[:, :, blocks[c]].rearrange("p t j -> p j t"))
+        th_woven = [sb("th_woven%d" % c, [P, P, PACK], F32) for c in range(len(blocks))]
+        for c, cols in enumerate(blocks):
+            nc.scalar.activation(th_woven[c][:], diff[:, :, cols].rearrange("p t j -> p j t"), ACT.Tanh)
 
         dw_picked = gather("dw_picked", dw_table[:].bitcast(U32), k1_l, U32, "d_win1")
         dq_codes = sb("dq_codes", [P, H], U32)
@@ -188,7 +167,7 @@ def tile_picked_twqjointbpolar_none_p_kernel(
         def multiply(c):
             nc.vector.tensor_tensor(
                 z_bf[:, c * P * PACK : (c + 1) * P * PACK].rearrange("p (j t) -> p j t", t=PACK),
-                th_ps[c][:].rearrange("p (t j) -> p j t", t=PACK),
+                th_woven[c][:],
                 yg_woven[c][:],
                 ALU.mult,
             )

@@ -15,6 +15,9 @@ ACT = mybir.ActivationFunctionType
 K, T, S, H, G, W = 512, 1024, 512, 512, 2048, 256
 P = 128
 PACK = 4
+GROUP = 16
+RUN = 8
+HALF = S // 2
 FLOPS = 3 * 2 * K * H * S
 
 
@@ -26,31 +29,69 @@ def tile_picked_twqjointbpolar_none_p_kernel(
         keep = ctx.enter_context(tc.tile_pool(name="keep", bufs=1))
         psum = ctx.enter_context(tc.psum_pool(name="psum", bufs=1))
 
-        def sb(name, shape, dtype, tag=""):
-            return keep.tile(shape, dtype, name=name, tag=tag, align_bytes=64)
+        def sbuf(name, shape, dtype, on=""):
+            return keep.tile(shape, dtype, name=name, tag=on or name, align_bytes=64)
 
-        def load_list(name, src):
-            tile = keep.tile(list(src.shape), U16, name=name)
-            nc.sync.dma_start(tile[:], src)
+        def bank(name, number):
+            return psum.tile([P, S], F32, name=name, tag="bank%d" % number)
+
+        def load_list(name, source):
+            tile = keep.tile(list(source.shape), U16, name=name)
+            nc.sync.dma_start(tile[:], source)
             return tile
 
-        def load_half(name, w, half):
-            raw = sb(name, [P, PACK, H // 2], F32)
-            cols = slice(half * H // 2, (half + 1) * H // 2)
-            nc.sync.dma_start(raw[:], w[:, cols].rearrange("(p j) c -> p j c", j=PACK))
-            return raw
+        def load_words(name, words):
+            tile = sbuf(name, [P, words.shape[2]], I32)
+            nc.sync.dma_start(tile[:], words[0].rearrange("p n j -> p (n j)").bitcast(I32))
+            return tile
 
-        xs_table = sb("xs_table", [P, T], U8)
-        nc.vector.memset(xs_table[:].bitcast(I32), 0)
-        ds_table = sb("ds_table", [P, G], U8)
-        nc.vector.memset(ds_table[:].bitcast(I32), 0)
-        dq_scales = sb("dq_scales", [P, H], U8)
-        nc.vector.memset(dq_scales[:].bitcast(I32), 0)
-        d_win = [sb("d_win%d" % a, [P, 2 * S], F32, "d_win%d" % a) for a in range(2)]
-        for win in d_win:
-            nc.vector.memset(win[:, S:], 0.0)
-        sq_win = [sb("sq_win%d" % a, [P, S], F32) for a in range(2)]
-        for win in sq_win:
+        def load_weights(name, w):
+            halves = []
+            for half in range(2):
+                raw = sbuf("%s_raw%d" % (name, half), [P, PACK, H // 2], F32)
+                nc.sync.dma_start(raw[:], w[:, half * H // 2 : (half + 1) * H // 2].rearrange("(p j) c -> p j c", j=PACK))
+                halves.append(raw)
+            return halves
+
+        def quantise_weights(name, halves):
+            rounded = sbuf(name + "_bf", [P, H * PACK], BF16)
+            dealt = rounded[:].rearrange("p (t m j) -> p m j t", t=PACK, j=PACK)
+            for half, raw in enumerate(halves):
+                nc.scalar.copy(dealt[:, half * P // 2 : (half + 1) * P // 2], raw[:].rearrange("p j (m t) -> p m j t", t=PACK))
+            codes = sbuf(name + "_codes", [P, H], U32)
+            scales = sbuf(name + "_scales", [P, H], U8)
+            nc.vector.quantize_mx(out=codes[:].bitcast(FP8X4), scales=scales[:], in_=rounded[:])
+            return codes, scales
+
+        def gather(name, window, entries, dtype, on=""):
+            picked = sbuf(name, [P, entries.shape[1] * GROUP], dtype, on)
+            nc.vector.tensor_copy(picked[:], window.indirect(entries))
+            return picked
+
+        def deal(dealt, picked, run):
+            nc.vector.tensor_copy(
+                dealt.rearrange("p (t a b) -> p t a b", t=PACK, b=run), picked.rearrange("p (a t b) -> p t a b", t=PACK, b=run)
+            )
+
+        def product(acc, stationary, t, codes, scales):
+            cols = slice(t * P, (t + 1) * P)
+            nc.tensor.matmul_mx(
+                out=acc,
+                lhsT=stationary[0][:, cols].bitcast(FP8X4),
+                lhsT_scale=stationary[1][:, cols],
+                rhs=codes.bitcast(FP8X4),
+                rhs_scale=scales,
+                start=True,
+                stop=True,
+            )
+
+        xs_table = sbuf("xs_table", [P, T], U8)
+        ds_table = sbuf("ds_table", [P, G], U8)
+        dq_scales = sbuf("dq_scales", [P, H], U8)
+        for plane in (xs_table, ds_table, dq_scales):
+            nc.vector.memset(plane[:].bitcast(I32), 0)
+        square_win = [sbuf("square_win%d" % a, [P, S], F32) for a in range(2)]
+        for win in square_win:
             nc.vector.memset(win[:], 0.0)
 
         two_l = load_list("two_l", two)
@@ -58,165 +99,122 @@ def tile_picked_twqjointbpolar_none_p_kernel(
         for q in range(4):
             queue = nc.sync if q < 2 else nc.scalar
             queue.dma_start(xs_table[32 * q : 32 * q + 4, :].bitcast(I32), x_scales[0, 4 * q : 4 * q + 4, :].bitcast(I32))
-        xw_table = sb("xw_table", [P, T], I32)
-        nc.sync.dma_start(xw_table[:], x_words[0].rearrange("p n t -> p (n t)").bitcast(I32))
-        w2_raw = [load_half("w2_raw%d" % a, w2, a) for a in range(2)]
+        xw_table = load_words("xw_table", x_words)
+        w2_raw = load_weights("w2", w2)
         k1_l = load_list("k1_l", k1)
         for e in range(2):
-            nc.sync.dma_start(ds_table[e:P:16, :].bitcast(I32), d_scales[0, e:16:2, :].bitcast(I32))
-        w1_raw = [load_half("w1_raw%d" % a, w1, a) for a in range(2)]
+            nc.sync.dma_start(ds_table[e:P:GROUP, :].bitcast(I32), d_scales[0, e:16:2, :].bitcast(I32))
+        w1_raw = load_weights("w1", w1)
         n2_l = load_list("n2_l", n2)
         n1_l = load_list("n1_l", n1)
-        gs_t = sb("gs_t", [P, PACK], F32)
+        gs_t = sbuf("gs_t", [P, PACK], F32)
         nc.sync.dma_start(gs_t[:], gs.rearrange("(p t) o -> p (t o)", t=PACK))
-        dw_table = sb("dw_table", [P, G], I32)
-        nc.sync.dma_start(dw_table[:], d_words[0].rearrange("p n t -> p (n t)").bitcast(I32))
+        dw_table = load_words("dw_table", d_words)
         n3_l = load_list("n3_l", n3)
         n4_l = load_list("n4_l", n4)
 
-        def round_weights(name, raws):
-            grouped = sb(name, [P, H * PACK], BF16, name)
-            view = grouped[:].rearrange("p (t m j) -> p m j t", t=PACK, j=PACK)
-            for half, raw in enumerate(raws):
-                nc.scalar.copy(view[:, half * 64 : (half + 1) * 64], raw[:].rearrange("p j (m t) -> p m j t", t=PACK))
-            return grouped
-
-        def quantise(name, values):
-            n = values.shape[1] // PACK
-            codes = sb(name + "_codes", [P, n], U32)
-            scales = sb(name + "_scales", [P, n], U8)
-            nc.vector.quantize_mx(out=codes[:].bitcast(FP8X4), scales=scales[:], in_=values[:])
-            return codes, scales
-
-        def gather(name, table, lst, dtype, tag=""):
-            picked = sb(name, [P, lst.shape[1] * 16], dtype, tag)
-            nc.vector.tensor_copy(picked[:], table.indirect(lst[:]))
-            return picked
-
-        def product(acc, lhs, t, rhs):
-            cols = slice(t * P, (t + 1) * P)
-            nc.tensor.matmul_mx(
-                out=acc,
-                lhsT=lhs[0][:, cols].bitcast(FP8X4),
-                lhsT_scale=lhs[1][:, cols],
-                rhs=rhs[0].bitcast(FP8X4),
-                rhs_scale=rhs[1],
-                start=True,
-                stop=True,
-            )
-
-        def bank(name, b):
-            return psum.tile([P, S], F32, name=name, tag="bank%d" % b)
-
-        xs_two = gather("xs_two", xs_table[:], two_l, U8)
-        xs_offs = gather("xs_offs", xs_table[:], offs_l, U8)
-        xw_two = gather("xw_two", xw_table[:].bitcast(U32), two_l, U32)
-        xw_offs = gather("xw_offs", xw_table[:].bitcast(U32), offs_l, U32)
-        w2_q = quantise("w2", round_weights("w2_bf", w2_raw))
+        xs_two = gather("xs_two", xs_table[:], two_l[:], U8)
+        xs_offs = gather("xs_offs", xs_table[:], offs_l[:], U8)
+        xw_two = gather("xw_two", xw_table[:].bitcast(U32), two_l[:], U32)
+        xw_offs = gather("xw_offs", xw_table[:].bitcast(U32), offs_l[:], U32)
+        w2_q = quantise_weights("w2", w2_raw)
         d_ps = [bank("d_ps%d" % t, t) for t in range(PACK)]
         for t in range(PACK):
-            product(d_ps[t][:], w2_q, t, (xw_two[:], xs_two[:]))
+            product(d_ps[t][:], w2_q, t, xw_two[:], xs_two[:])
 
-        ds_picked = gather("ds_picked", ds_table[:], k1_l, U8, "w2_bf")
-        ds_dealt = sb("ds_dealt", [P, H], U8)
-        nc.vector.tensor_copy(
-            ds_dealt[:].bitcast(I32).rearrange("p (t a b) -> p t a b", t=PACK, b=2),
-            ds_picked[:].bitcast(I32).rearrange("p (a t b) -> p t a b", t=PACK, b=2),
-        )
+        ds_picked = gather("ds_picked", ds_table[:], k1_l[:], U8, on="w2_raw1")
+        ds_dealt = sbuf("ds_dealt", [P, H], U8)
+        deal(ds_dealt[:].bitcast(I32), ds_picked[:].bitcast(I32), RUN // 4)
         for odd in range(2):
             for e in range(2):
-                nc.sync.dma_start(dq_scales[2 * odd + e : P : 32, :].bitcast(I32), ds_dealt[16 * odd + e : P : 32, :].bitcast(I32))
+                nc.sync.dma_start(
+                    dq_scales[2 * odd + e : P : 32, :].bitcast(I32), ds_dealt[GROUP * odd + e : P : 32, :].bitcast(I32)
+                )
 
-        w1_q = quantise("w1", round_weights("w1_bf", w1_raw))
-        for t in range(2):
-            nc.scalar.copy(d_win[t][:, :S], d_ps[t][:])
-        yg = sb("yg", [P, PACK, S], F32)
+        w1_q = quantise_weights("w1", w1_raw)
+        d_win = [sbuf("d_win%d" % t, [P, S], F32) for t in range(PACK)]
+        for t in range(PACK):
+            nc.scalar.copy(d_win[t][:], d_ps[t][:])
+        yg = sbuf("yg", [P, PACK, S], F32)
         for t in range(PACK):
             y_ps = bank("y_ps%d" % t, PACK + t)
-            product(y_ps[:], w1_q, t, (xw_offs[:], xs_offs[:]))
+            product(y_ps[:], w1_q, t, xw_offs[:], xs_offs[:])
             nc.scalar.activation(yg[:, t, :], y_ps[:], ACT.Copy, scale=gs_t[:, t : t + 1])
+        blocks = range(S // P)
+        yg_woven = [sbuf("yg_woven%d" % c, [P, P, PACK], F32) for c in blocks]
+        for c in blocks:
+            nc.scalar.copy(yg_woven[c][:], yg[:, :, c * P : (c + 1) * P].rearrange("p t j -> p j t"))
 
-        blocks = [slice(c, c + P) for c in range(0, S, P)]
-        yg_woven = [sb("yg_woven%d" % c, [P, P, PACK], F32) for c in range(len(blocks))]
-        diff = sb("diff", [P, PACK, S], F32)
+        halves = [slice(u * HALF // GROUP, (u + 1) * HALF // GROUP) for u in range(2)]
+        diff = [sbuf("diff%d" % u, [P, PACK, HALF], F32) for u in range(2)]
         for t in range(PACK):
-            win = d_win[t % 2]
-            d2 = gather("d2_%d" % t, win[:], n2_l, F32)
-            nc.vector.tensor_tensor(diff[:, t, :], win[:].indirect(n1_l[:]), d2[:], ALU.subtract)
-            if t + 2 < PACK:
-                nc.scalar.copy(win[:, :S], d_ps[t + 2][:])
-                for c in (2 * t, 2 * t + 1):
-                    nc.scalar.copy(yg_woven[c][:], yg[:, :, blocks[c]].rearrange("p t j -> p j t"))
-        th_woven = [sb("th_woven%d" % c, [P, P, PACK], F32) for c in range(len(blocks))]
-        for c, cols in enumerate(blocks):
-            nc.scalar.activation(th_woven[c][:], diff[:, :, cols].rearrange("p t j -> p j t"), ACT.Tanh)
+            d_n2 = [gather("d_n2_%d_%d" % (t, u), d_win[t][:], n2_l[:, halves[u]], F32) for u in range(2)]
+            for u in range(2):
+                nc.vector.tensor_tensor(diff[u][:, t, :], d_win[t][:].indirect(n1_l[:, halves[u]]), d_n2[u][:], ALU.subtract)
+        tanh_woven = sbuf("tanh_woven", [P, S, PACK], F32, on="yg")
+        for c in blocks:
+            u, start = divmod(c * P, HALF)
+            woven_read = diff[u][:, :, start : start + P].rearrange("p t j -> p j t")
+            nc.scalar.activation(tanh_woven[:, c * P : (c + 1) * P, :], woven_read, ACT.Tanh)
 
-        dw_picked = gather("dw_picked", dw_table[:].bitcast(U32), k1_l, U32, "d_win1")
-        dq_codes = sb("dq_codes", [P, H], U32)
-        nc.vector.tensor_copy(
-            dq_codes[:].rearrange("p (t a b) -> p t a b", t=PACK, b=8),
-            dw_picked[:].rearrange("p (a t b) -> p t a b", t=PACK, b=8),
-        )
-
-        z_bf = sb("z_bf", [P, S * PACK], BF16)
-        z_codes = sb("z_codes", [P, S], U32)
-        z_scales = sb("z_scales", [P, S], U8)
-        h_win = [sb("h_win%d" % t, [P, S], F32) for t in range(PACK)]
+        dw_picked = gather("dw_picked", dw_table[:].bitcast(U32), k1_l[:], U32, on="d_n2_%d_0" % (PACK - 1))
+        dq_codes = sbuf("dq_codes", [P, H], U32)
+        deal(dq_codes[:], dw_picked[:], RUN)
         dq = (dq_codes, dq_scales)
 
-        def multiply(c):
-            nc.vector.tensor_tensor(
-                z_bf[:, c * P * PACK : (c + 1) * P * PACK].rearrange("p (j t) -> p j t", t=PACK),
-                th_woven[c][:],
-                yg_woven[c][:],
-                ALU.mult,
-            )
+        z_bf = sbuf("z_bf", [P, S * PACK], BF16)
+        z_codes = sbuf("z_codes", [P, S], U32)
+        z_scales = sbuf("z_scales", [P, S], U8)
+        h_win = [sbuf("h_win%d" % t, [P, S], F32) for t in range(PACK)]
 
-        def first_rows(n, lo, hi):
-            nc.vector.quantize_mx(out=z_codes[:, lo:hi].bitcast(FP8X4), scales=z_scales[:, lo:hi], in_=z_bf[:, lo * PACK : hi * PACK])
-            acc = bank("h0_ps%d" % n, PACK + n)
-            product(acc[:, : hi - lo], dq, 0, (z_codes[:, lo:hi], z_scales[:, lo:hi]))
+        def multiply(c):
+            z_block = z_bf[:, c * P * PACK : (c + 1) * P * PACK].rearrange("p (j t) -> p j t", t=PACK)
+            nc.vector.tensor_tensor(z_block, tanh_woven[:, c * P : (c + 1) * P, :], yg_woven[c][:], ALU.mult)
+
+        def quantise_z(piece, lo, hi):
+            nc.vector.quantize_mx(
+                out=z_codes[:, lo:hi].bitcast(FP8X4), scales=z_scales[:, lo:hi], in_=z_bf[:, lo * PACK : hi * PACK]
+            )
+            acc = bank("h0_ps%d" % piece, PACK + piece)
+            product(acc[:, : hi - lo], dq, 0, z_codes[:, lo:hi], z_scales[:, lo:hi])
             nc.scalar.activation(h_win[0][:, lo:hi], acc[:, : hi - lo], ACT.Copy, scale=0.0625)
 
         for c in range(3):
             multiply(c)
-        first_rows(0, 0, 2 * P)
+        quantise_z(0, 0, 2 * P)
         multiply(3)
-        first_rows(1, 2 * P, 3 * P)
-        first_rows(2, 3 * P, 4 * P)
-        h_ps = [None] + [bank("h_ps%d" % t, t) for t in range(1, PACK)]
-        for t in range(1, PACK):
-            product(h_ps[t][:], dq, t, (z_codes[:], z_scales[:]))
+        quantise_z(1, 2 * P, 3 * P)
+        quantise_z(2, 3 * P, 4 * P)
+        h_ps = {t: bank("h_ps%d" % t, t) for t in range(1, PACK)}
+        for t in h_ps:
+            product(h_ps[t][:], dq, t, z_codes[:], z_scales[:])
 
-        out_v = out.rearrange("(a t b) n -> t a b n", t=PACK, b=8)
-        pairs = []
+        out_rows = out.rearrange("(a t b) n -> t a b n", t=PACK, b=RUN)
+        pairs, results = [], []
 
         def fetch(t):
-            if t > 0:
+            if t in h_ps:
                 nc.scalar.activation(h_win[t][:], h_ps[t][:], ACT.Copy, scale=0.0625)
-            half_a = sb("half_a%d" % t, [P, W], F32)
-            nc.vector.tensor_scalar(half_a[:], h_win[t][:].indirect(n3_l[:]), -0.5, 0.0, ALU.mult, ALU.add)
-            pb = gather("pb%d" % t, h_win[t][:], n4_l, F32)
-            pairs.append((half_a, pb))
-
-        results = []
+            minus_half_pa = sbuf("minus_half_pa%d" % t, [P, W], F32)
+            nc.vector.tensor_scalar(minus_half_pa[:], h_win[t][:].indirect(n3_l[:]), -0.5, 0.0, ALU.mult, ALU.add)
+            pairs.append((minus_half_pa, gather("pb%d" % t, h_win[t][:], n4_l[:], F32)))
 
         def root(t):
-            half_a, pb = pairs[t]
-            sq_a = sb("sq_a%d" % t, [P, W], F32)
-            sq_b = sb("sq_b%d" % t, [P, W], F32)
-            nc.scalar.activation(sq_a[:], half_a[:], ACT.Square, scale=2.0)
-            nc.scalar.activation(sq_b[:], pb[:], ACT.Square)
-            win = sq_win[t % 2]
-            nc.vector.tensor_tensor(win[:].indirect(n3_l[:]), sq_a[:], sq_b[:], ALU.add)
-            res = sb("res%d" % t, [P, S], F32)
-            nc.scalar.activation(res[:], win[:], ACT.Sqrt, bias=0.25)
-            results.append(res)
+            minus_half_pa, pb = pairs[t]
+            square_a = sbuf("square_a%d" % t, [P, W], F32)
+            square_b = sbuf("square_b%d" % t, [P, W], F32)
+            nc.scalar.activation(square_a[:], minus_half_pa[:], ACT.Square, scale=2.0)
+            nc.scalar.activation(square_b[:], pb[:], ACT.Square)
+            win = square_win[t % 2]
+            nc.vector.tensor_tensor(win[:].indirect(n3_l[:]), square_a[:], square_b[:], ALU.add)
+            result = sbuf("result%d" % t, [P, S], F32)
+            nc.scalar.activation(result[:], win[:], ACT.Sqrt, bias=0.25)
+            results.append(result)
 
         def finish(t):
-            half_a, pb = pairs[t]
-            nc.vector.tensor_tensor(results[t][:].indirect(n4_l[:]), pb[:], half_a[:], ALU.add)
-            nc.sync.dma_start(out_v[t], results[t][:])
+            minus_half_pa, pb = pairs[t]
+            nc.vector.tensor_tensor(results[t][:].indirect(n4_l[:]), pb[:], minus_half_pa[:], ALU.add)
+            nc.sync.dma_start(out_rows[t], results[t][:])
 
         for step in range(PACK + 2):
             if step < PACK:

from contextlib import ExitStack

import concourse.mybir as mybir

F32 = mybir.dt.float32
BF16 = mybir.dt.bfloat16
I32 = mybir.dt.int32
U32 = mybir.dt.uint32
U16 = mybir.dt.uint16
U8 = mybir.dt.uint8
FP8X4 = mybir.dt.float8_e4m3fn_x4
ALU = mybir.AluOpType
ACT = mybir.ActivationFunctionType

K, T, S, H, G, W = 512, 1024, 512, 512, 2048, 256
P = 128
PACK = 4
GROUP = 16
RUN = 8
HALF = S // 2
FLOPS = 3 * 2 * K * H * S


def tile_picked_twqjointbpolar_none_p_kernel(
    tc, x_words, x_scales, w1, w2, gs, d_words, d_scales, offs, two, n1, n2, k1, n3, n4, out
):
    nc = tc.nc
    with ExitStack() as ctx:
        keep = ctx.enter_context(tc.tile_pool(name="keep", bufs=1))
        psum = ctx.enter_context(tc.psum_pool(name="psum", bufs=1))

        def sbuf(name, shape, dtype, on=""):
            return keep.tile(shape, dtype, name=name, tag=on or name, align_bytes=64)

        def bank(name, number):
            return psum.tile([P, S], F32, name=name, tag="bank%d" % number)

        def load_list(name, source):
            tile = keep.tile(list(source.shape), U16, name=name)
            nc.sync.dma_start(tile[:], source)
            return tile

        def load_words(name, words):
            tile = sbuf(name, [P, words.shape[2]], I32)
            nc.sync.dma_start(tile[:], words[0].rearrange("p n j -> p (n j)").bitcast(I32))
            return tile

        def load_weights(name, w):
            halves = []
            for half in range(2):
                raw = sbuf("%s_raw%d" % (name, half), [P, PACK, H // 2], F32)
                nc.sync.dma_start(raw[:], w[:, half * H // 2 : (half + 1) * H // 2].rearrange("(p j) c -> p j c", j=PACK))
                halves.append(raw)
            return halves

        def quantise_weights(name, halves):
            rounded = sbuf(name + "_bf", [P, H * PACK], BF16)
            dealt = rounded[:].rearrange("p (t m j) -> p m j t", t=PACK, j=PACK)
            for half, raw in enumerate(halves):
                nc.scalar.copy(dealt[:, half * P // 2 : (half + 1) * P // 2], raw[:].rearrange("p j (m t) -> p m j t", t=PACK))
            codes = sbuf(name + "_codes", [P, H], U32)
            scales = sbuf(name + "_scales", [P, H], U8)
            nc.vector.quantize_mx(out=codes[:].bitcast(FP8X4), scales=scales[:], in_=rounded[:])
            return codes, scales

        def gather(name, window, entries, dtype, on=""):
            picked = sbuf(name, [P, entries.shape[1] * GROUP], dtype, on)
            nc.vector.tensor_copy(picked[:], window.indirect(entries))
            return picked

        def deal(dealt, picked, run):
            nc.vector.tensor_copy(
                dealt.rearrange("p (t a b) -> p t a b", t=PACK, b=run), picked.rearrange("p (a t b) -> p t a b", t=PACK, b=run)
            )

        def product(acc, stationary, t, codes, scales):
            cols = slice(t * P, (t + 1) * P)
            nc.tensor.matmul_mx(
                out=acc,
                lhsT=stationary[0][:, cols].bitcast(FP8X4),
                lhsT_scale=stationary[1][:, cols],
                rhs=codes.bitcast(FP8X4),
                rhs_scale=scales,
                start=True,
                stop=True,
            )

        xs_table = sbuf("xs_table", [P, T], U8)
        ds_table = sbuf("ds_table", [P, G], U8)
        dq_scales = sbuf("dq_scales", [P, H], U8)
        for plane in (xs_table, ds_table, dq_scales):
            nc.vector.memset(plane[:].bitcast(I32), 0)
        square_win = [sbuf("square_win%d" % a, [P, S], F32) for a in range(2)]
        for win in square_win:
            nc.vector.memset(win[:], 0.0)

        two_l = load_list("two_l", two)
        offs_l = load_list("offs_l", offs)
        for q in range(4):
            queue = nc.sync if q < 2 else nc.scalar
            queue.dma_start(xs_table[32 * q : 32 * q + 4, :].bitcast(I32), x_scales[0, 4 * q : 4 * q + 4, :].bitcast(I32))
        xw_table = load_words("xw_table", x_words)
        w2_raw = load_weights("w2", w2)
        k1_l = load_list("k1_l", k1)
        for e in range(2):
            nc.sync.dma_start(ds_table[e:P:GROUP, :].bitcast(I32), d_scales[0, e:16:2, :].bitcast(I32))
        w1_raw = load_weights("w1", w1)
        n2_l = load_list("n2_l", n2)
        n1_l = load_list("n1_l", n1)
        gs_t = sbuf("gs_t", [P, PACK], F32)
        nc.sync.dma_start(gs_t[:], gs.rearrange("(p t) o -> p (t o)", t=PACK))
        dw_table = load_words("dw_table", d_words)
        n3_l = load_list("n3_l", n3)
        n4_l = load_list("n4_l", n4)

        xs_two = gather("xs_two", xs_table[:], two_l[:], U8)
        xs_offs = gather("xs_offs", xs_table[:], offs_l[:], U8)
        xw_two = gather("xw_two", xw_table[:].bitcast(U32), two_l[:], U32)
        xw_offs = gather("xw_offs", xw_table[:].bitcast(U32), offs_l[:], U32)
        w2_q = quantise_weights("w2", w2_raw)
        d_ps = [bank("d_ps%d" % t, t) for t in range(PACK)]
        for t in range(PACK):
            product(d_ps[t][:], w2_q, t, xw_two[:], xs_two[:])

        ds_picked = gather("ds_picked", ds_table[:], k1_l[:], U8, on="w2_raw1")
        ds_dealt = sbuf("ds_dealt", [P, H], U8)
        deal(ds_dealt[:].bitcast(I32), ds_picked[:].bitcast(I32), RUN // 4)
        for odd in range(2):
            for e in range(2):
                nc.sync.dma_start(
                    dq_scales[2 * odd + e : P : 32, :].bitcast(I32), ds_dealt[GROUP * odd + e : P : 32, :].bitcast(I32)
                )

        w1_q = quantise_weights("w1", w1_raw)
        d_win = [sbuf("d_win%d" % t, [P, S], F32) for t in range(PACK)]
        for t in range(PACK):
            nc.scalar.copy(d_win[t][:], d_ps[t][:])
        yg = sbuf("yg", [P, PACK, S], F32)
        for t in range(PACK):
            y_ps = bank("y_ps%d" % t, PACK + t)
            product(y_ps[:], w1_q, t, xw_offs[:], xs_offs[:])
            nc.scalar.activation(yg[:, t, :], y_ps[:], ACT.Copy, scale=gs_t[:, t : t + 1])
        blocks = range(S // P)
        yg_woven = [sbuf("yg_woven%d" % c, [P, P, PACK], F32) for c in blocks]
        for c in blocks:
            nc.scalar.copy(yg_woven[c][:], yg[:, :, c * P : (c + 1) * P].rearrange("p t j -> p j t"))

        halves = [slice(u * HALF // GROUP, (u + 1) * HALF // GROUP) for u in range(2)]
        diff = [sbuf("diff%d" % u, [P, PACK, HALF], F32) for u in range(2)]
        for t in range(PACK):
            d_n2 = [gather("d_n2_%d_%d" % (t, u), d_win[t][:], n2_l[:, halves[u]], F32) for u in range(2)]
            for u in range(2):
                nc.vector.tensor_tensor(diff[u][:, t, :], d_win[t][:].indirect(n1_l[:, halves[u]]), d_n2[u][:], ALU.subtract)
        tanh_woven = sbuf("tanh_woven", [P, S, PACK], F32, on="yg")
        for c in blocks:
            u, start = divmod(c * P, HALF)
            woven_read = diff[u][:, :, start : start + P].rearrange("p t j -> p j t")
            nc.scalar.activation(tanh_woven[:, c * P : (c + 1) * P, :], woven_read, ACT.Tanh)

        dw_picked = gather("dw_picked", dw_table[:].bitcast(U32), k1_l[:], U32, on="d_n2_%d_0" % (PACK - 1))
        dq_codes = sbuf("dq_codes", [P, H], U32)
        deal(dq_codes[:], dw_picked[:], RUN)
        dq = (dq_codes, dq_scales)

        z_bf = sbuf("z_bf", [P, S * PACK], BF16)
        z_codes = sbuf("z_codes", [P, S], U32)
        z_scales = sbuf("z_scales", [P, S], U8)
        h_win = [sbuf("h_win%d" % t, [P, S], F32) for t in range(PACK)]

        def multiply(c):
            z_block = z_bf[:, c * P * PACK : (c + 1) * P * PACK].rearrange("p (j t) -> p j t", t=PACK)
            nc.vector.tensor_tensor(z_block, tanh_woven[:, c * P : (c + 1) * P, :], yg_woven[c][:], ALU.mult)

        def quantise_z(piece, lo, hi):
            nc.vector.quantize_mx(
                out=z_codes[:, lo:hi].bitcast(FP8X4), scales=z_scales[:, lo:hi], in_=z_bf[:, lo * PACK : hi * PACK]
            )
            acc = bank("h0_ps%d" % piece, PACK + piece)
            product(acc[:, : hi - lo], dq, 0, z_codes[:, lo:hi], z_scales[:, lo:hi])
            nc.scalar.activation(h_win[0][:, lo:hi], acc[:, : hi - lo], ACT.Copy, scale=0.0625)

        for c in range(3):
            multiply(c)
        quantise_z(0, 0, 2 * P)
        multiply(3)
        quantise_z(1, 2 * P, 3 * P)
        quantise_z(2, 3 * P, 4 * P)
        h_ps = {t: bank("h_ps%d" % t, t) for t in range(1, PACK)}
        for t in h_ps:
            product(h_ps[t][:], dq, t, z_codes[:], z_scales[:])

        out_rows = out.rearrange("(a t b) n -> t a b n", t=PACK, b=RUN)
        pairs, results = [], []

        def fetch(t):
            if t in h_ps:
                nc.scalar.activation(h_win[t][:], h_ps[t][:], ACT.Copy, scale=0.0625)
            minus_half_pa = sbuf("minus_half_pa%d" % t, [P, W], F32)
            nc.vector.tensor_scalar(minus_half_pa[:], h_win[t][:].indirect(n3_l[:]), -0.5, 0.0, ALU.mult, ALU.add)
            pairs.append((minus_half_pa, gather("pb%d" % t, h_win[t][:], n4_l[:], F32)))

        def root(t):
            minus_half_pa, pb = pairs[t]
            square_a = sbuf("square_a%d" % t, [P, W], F32)
            square_b = sbuf("square_b%d" % t, [P, W], F32)
            nc.scalar.activation(square_a[:], minus_half_pa[:], ACT.Square, scale=2.0)
            nc.scalar.activation(square_b[:], pb[:], ACT.Square)
            win = square_win[t % 2]
            nc.vector.tensor_tensor(win[:].indirect(n3_l[:]), square_a[:], square_b[:], ALU.add)
            result = sbuf("result%d" % t, [P, S], F32)
            nc.scalar.activation(result[:], win[:], ACT.Sqrt, bias=0.25)
            results.append(result)

        def finish(t):
            minus_half_pa, pb = pairs[t]
            nc.vector.tensor_tensor(results[t][:].indirect(n4_l[:]), pb[:], minus_half_pa[:], ALU.add)
            nc.sync.dma_start(out_rows[t], results[t][:])

        for step in range(PACK + 2):
            if step < PACK:
                fetch(step)
            if 1 <= step <= PACK:
                root(step - 1)
            if step >= 2:
                finish(step - 2)
